import numpy as np
import ml_dtypes


def mxq(x, axis, fmt="e4m3"):
    dtype, down = {"e4m3": (ml_dtypes.float8_e4m3fn, 7), "e5m2": (ml_dtypes.float8_e5m2, 14)}[fmt]
    v = np.moveaxis(np.asarray(x, np.float32).astype(ml_dtypes.bfloat16).astype(np.float64), axis, -1)
    blocks = v.reshape(v.shape[:-1] + (-1, 32))
    amax = np.abs(blocks).max(-1, keepdims=True)
    byte = np.maximum(np.where(amax > 0, np.frexp(amax)[1] - 1 + 127, 0) - down, 1)
    scale = np.exp2(byte - 127.0)
    codes = (blocks / scale).astype(np.float32).astype(dtype).astype(np.float64)
    return np.moveaxis((codes * scale).reshape(v.shape), -1, axis)


WIDE = False


def mx_kscale(k):
    if not WIDE:
        return np.ones(k)
    levels = np.array([30, -30])
    if k % 512:
        return np.exp2(np.random.permutation(np.resize(levels, k // 32))).repeat(32)
    a = np.empty((k // 512, 16))
    for p in range(k // 512):
        a[p, :8] = np.random.permutation(np.resize(levels, 8))
        for g in range(8):
            far = levels[np.abs(levels - a[p, g]) >= 10]
            a[p, g + 8] = far[np.random.randint(len(far))]
    return np.exp2(a.ravel()).repeat(32)


BF16 = ml_dtypes.bfloat16


def bf(x):
    return np.asarray(x, np.float32).astype(BF16)


def f64(x):
    return np.asarray(x).astype(np.float64)


E2M1 = np.array([0.0, 0.5, 1.0, 1.5, 2.0, 3.0, 4.0, 6.0, -0.0, -0.5, -1.0, -1.5, -2.0, -3.0, -4.0, -6.0])


def pack_weight(w, fmt):
    k, n = w.shape
    w = f64(bf(w)).reshape(k // 32, 32, n)
    amax = np.abs(w).max(1)
    if fmt in ("e4m3", "e5m2"):
        byte = np.frexp(amax)[1] - 1 + 127 - (7 if fmt == "e4m3" else 14)
    else:
        mant, ex = np.frexp(amax / 6.0)
        byte = np.where(mant > 0.5, ex, ex - 1) + 127
    byte = np.clip(np.where(amax > 0, byte, 1), 1, 254)
    scaled = (w * np.exp2(127.0 - byte)[:, None, :]).reshape(k, n).astype(np.float32)
    by_word = np.ascontiguousarray(scaled.reshape(k // 512, 128, 4, n).transpose(0, 1, 3, 2))
    if fmt in ("e4m3", "e5m2"):
        words = by_word.astype(ml_dtypes.float8_e4m3fn if fmt == "e4m3" else ml_dtypes.float8_e5m2).view(np.uint8)
    else:
        c = by_word.astype(ml_dtypes.float4_e2m1fn).view(np.uint8) & 0xF
        words = c[..., 0::2] | (c[..., 1::2] << 4)
    return np.ascontiguousarray(words), np.ascontiguousarray(byte.astype(np.uint8).reshape(k // 512, 16, n))


def unpack_weight(words, scales, fmt):
    g, p, n, _ = words.shape
    if fmt in ("e4m3", "e5m2"):
        vals = np.ascontiguousarray(words).view(ml_dtypes.float8_e4m3fn if fmt == "e4m3" else ml_dtypes.float8_e5m2).astype(np.float64)
    else:
        nib = np.empty((g, p, n, 4), np.uint8)
        nib[..., 0::2] = words & 0xF
        nib[..., 1::2] = words >> 4
        vals = E2M1[nib]
    vals = vals * np.repeat(np.exp2(scales.astype(np.float64) - 127.0), 8, axis=1)[..., None]
    return vals.transpose(0, 1, 3, 2).reshape(g * 512, n)


K, N, R, S = 2048, 1024, 1024, 2048


def setup_inputs():
    s = mx_kscale(K)
    t = mx_kscale(R)
    G = np.random.standard_normal((K, N)) * np.exp(0.5 * np.random.standard_normal((K, N)))
    innov_words, innov_scales = pack_weight(G * s[:, None], "e5m2")
    return {
        "innov_words": innov_words,
        "innov_scales": innov_scales,
        "obs_modes": bf(np.random.standard_normal((K, R)) / np.sqrt(K) / s[:, None] * t),
        "mode_ratio": bf(np.random.uniform(0.2, 4.0, R)),
        "state_modes": bf(np.random.standard_normal((S, R)) / np.sqrt(R) / t),
    }


def reference(innov_words, innov_scales, obs_modes, mode_ratio, state_modes):
    G = unpack_weight(innov_words, innov_scales, "e5m2")
    U = mxq(f64(obs_modes), 0, "e4m3")
    z = U.T @ G
    r = f64(mode_ratio)
    gain = r / (1.0 + r * r)
    h = mxq(z * gain[:, None], 0, "e5m2")
    V = mxq(f64(state_modes), 1, "e4m3")
    return V @ h

@@ -1,0 +1,255 @@
+from contextlib import ExitStack
+
+import concourse.mybir as mybir
+from concourse.masks import make_identity
+
+K, N, R, S = 2048, 1024, 1024, 2048
+FLOPS = 2 * K * R * N + 2 * S * R * N
+
+F32 = mybir.dt.float32
+BF16 = mybir.dt.bfloat16
+U32 = mybir.dt.uint32
+I32 = mybir.dt.int32
+U8 = mybir.dt.uint8
+E4 = mybir.dt.float8_e4m3fn_x4
+E5 = mybir.dt.float8_e5m2_x4
+COPY = mybir.ActivationFunctionType.Copy
+MULT = mybir.AluOpType.mult
+
+P = 128
+KG = K // 512
+ST = S // P
+SP = ST // 2
+
+
+def tile_factored_gain_correction_e3_kernel(tc, innov_words, innov_scales, obs_modes, mode_ratio, state_modes, out):
+    nc = tc.nc
+    v_rows = state_modes.rearrange("(p a) r -> p a r", a=ST)
+    out_rows = out.rearrange("(p a) n -> p a n", a=ST)
+
+    with ExitStack() as ctx:
+        keep = ctx.enter_context(tc.tile_pool(name="keep", bufs=1))
+        work = ctx.enter_context(tc.tile_pool(name="work", bufs=2))
+        psum = ctx.enter_context(tc.psum_pool(name="psum", bufs=1))
+        ctx.enter_context(tc.manual_schedule())
+
+        def bank(b):
+            return psum.tile([P, 512], F32, name="bank%d" % b, tag="bank%d" % b)
+
+        ident = keep.tile([P, P], F32, name="ident", align_bytes=64)
+        ratio = keep.tile([P, 2, 4], BF16, name="ratio")
+        square = keep.tile([P, 8], F32, name="square")
+        gain = keep.tile([P, 8], F32, name="gain")
+        g_words = [keep.tile([P, N], U32, name="g_words%d" % g, align_bytes=64) for g in range(KG)]
+        g_scales = keep.tile([P, KG, N], U8, name="g_scales", align_bytes=64)
+        u_raw = {(g, r): keep.tile([P, 4, 512], BF16, name="u_raw%d_%d" % (g, r), align_bytes=64) for g in range(KG) for r in range(2)}
+        u_codes = {k: keep.tile([P, 512], U32, name="u_codes%d_%d" % k, align_bytes=64) for k in u_raw}
+        u_scales = {k: keep.tile([P, 512], U8, name="u_scales%d_%d" % k, align_bytes=64) for k in u_raw}
+        v_raw = [keep.tile([P, 2, R], BF16, name="v_raw%d" % q, align_bytes=64) for q in range(SP)]
+        v_codes = [keep.tile([P, 512], U32, name="v_codes%d" % q, align_bytes=64) for q in range(SP)]
+        v_scales = [keep.tile([P, 512], U8, name="v_scales%d" % q, align_bytes=64) for q in range(SP)]
+        h_codes = {(r, n): keep.tile([P, 512], U32, name="h_codes%d_%d" % (r, n), align_bytes=64) for r in range(2) for n in range(2)}
+        h_scales = {k: keep.tile([P, 512], U8, name="h_scales%d_%d" % k, align_bytes=64) for k in h_codes}
+
+        make_identity(nc, ident[:])
+        nc.vector.memset(g_scales[:].rearrange("p g n -> p (g n)").bitcast(I32), 0)
+        nc.sync.dma_start(out=v_raw[0][:, 0:1, :], in_=v_rows[:, 0:1, :])
+        nc.sync.dma_start(out=v_raw[0][:, 1:2, :], in_=v_rows[:, 1:2, :])
+        nc.sync.dma_start(out=v_raw[1][:], in_=v_rows[:, 2:4, :])
+        nc.scalar.dma_start(out=ratio[:], in_=mode_ratio.rearrange("(g p t) -> p g t", g=2, t=4))
+        for q in range(4):
+            nc.scalar.dma_start(
+                out=g_scales[32 * q : 32 * q + 4, :, :].bitcast(I32),
+                in_=innov_scales[:, 4 * q : 4 * q + 4, :].rearrange("g q n -> q g n").bitcast(I32),
+            )
+
+        def load_u(g, r):
+            rows = obs_modes[512 * g : 512 * (g + 1), 512 * r : 512 * (r + 1)]
+            nc.sync.dma_start(out=u_raw[g, r][:], in_=rows.rearrange("(p j) w -> p j w", j=4))
+
+        for g in range(KG):
+            load_u(g, 0)
+            nc.sync.dma_start(out=g_words[g][:].bitcast(I32), in_=innov_words[g].rearrange("p n t -> p (n t)").bitcast(I32))
+        for g in range(KG):
+            load_u(g, 1)
+        for q in range(2, SP):
+            nc.sync.dma_start(out=v_raw[q][:], in_=v_rows[:, 2 * q : 2 * q + 2, :])
+
+        def make_gain():
+            flat = ratio[:].rearrange("p g t -> p (g t)")
+            nc.vector.tensor_tensor(out=square[:], in0=flat, in1=flat, op=MULT)
+            nc.vector.tensor_scalar_add(square[:], square[:], 1.0)
+            nc.vector.reciprocal(square[:], square[:])
+            nc.vector.tensor_tensor(out=gain[:], in0=flat, in1=square[:], op=MULT)
+
+        v_group = {}
+
+        def transpose_v(a, b):
+            words = v_raw[a // 2][:, a % 2, :].bitcast(F32)
+            t = bank(b)
+            for g in range(2):
+                for u in range(2):
+                    c = 2 * g + u
+                    nc.tensor.transpose(t[:, 128 * c : 128 * (c + 1)], words[:, 256 * g + u : 256 * (g + 1) : 2], ident[:])
+            return t
+
+        def empty_v(a, t, engine):
+            q = a // 2
+            if q not in v_group:
+                v_group[q] = work.tile([P, 2, 2, P, 4], BF16, name="v_group", tag="v_group", bufs=3, align_bytes=64)
+            dst = v_group[q][:, a % 2].rearrange("p g s t -> p g (s t)").bitcast(F32).rearrange("p g (s u) -> p g s u", u=2)
+            src = t[:].rearrange("p (g u s) -> p g s u", g=2, u=2)
+            if engine == "s":
+                nc.scalar.copy(out=dst, in_=src)
+            else:
+                nc.vector.tensor_copy(out=dst, in_=src)
+
+        def quantize_v(q):
+            nc.vector.quantize_mx(out=v_codes[q][:].bitcast(E4), scales=v_scales[q][:], in_=v_group[q][:].rearrange("p i g s t -> p (i g s t)"))
+
+        u_group = {}
+
+        def group_u(g, r, cut):
+            u_group[g, r] = work.tile([P, 4, P, 4], BF16, name="u_group", tag="u_group", bufs=3, align_bytes=64)
+            src = u_raw[g, r][:].rearrange("p j (m t) -> p t m j", t=4)
+            if cut < 4:
+                nc.scalar.copy(out=u_group[g, r][:, cut:4], in_=src[:, cut:4])
+            nc.vector.tensor_copy(out=u_group[g, r][:, 0:cut], in_=src[:, 0:cut])
+
+        def quantize_u(g, r):
+            nc.vector.quantize_mx(out=u_codes[g, r][:].bitcast(E4), scales=u_scales[g, r][:], in_=u_group[g, r][:].rearrange("p t m j -> p (t m j)"))
+
+        z = {}
+
+        def stage1(g, r, n, base):
+            cols = slice(512 * n, 512 * (n + 1))
+            for t in range(4):
+                if g == 0:
+                    z[r, n, t] = bank(base + t)
+                m = slice(128 * t, 128 * (t + 1))
+                nc.tensor.matmul_mx(
+                    out=z[r, n, t][:],
+                    lhsT=u_codes[g, r][:, m].bitcast(E4),
+                    lhsT_scale=u_scales[g, r][:, m],
+                    rhs=g_words[g][:, cols].bitcast(E5),
+                    rhs_scale=g_scales[:, g, cols],
+                    start=(g == 0),
+                    stop=(g == KG - 1),
+                )
+
+        h_rows = {}
+        h_group = {}
+
+        def empty_z(r, n, t, engine):
+            if (r, n) not in h_rows:
+                h_rows[r, n] = work.tile([P, 4, 512], BF16, name="h_rows", tag="h_rows", bufs=3, align_bytes=64)
+            scale = gain[:, 4 * r + t : 4 * r + t + 1]
+            if engine == "s":
+                nc.scalar.activation(out=h_rows[r, n][:, t, :], in_=z[r, n, t][:], func=COPY, scale=scale)
+            else:
+                nc.vector.tensor_scalar_mul(h_rows[r, n][:, t, :], z[r, n, t][:], scale)
+
+        def group_h(r, n, cut):
+            h_group[r, n] = work.tile([P, 512, 4], BF16, name="h_group", tag="h_group", bufs=2, align_bytes=64)
+            src = h_rows[r, n][:].rearrange("p t n -> p n t")
+            nc.vector.tensor_copy(out=h_group[r, n][:, 0:cut], in_=src[:, 0:cut])
+            if cut < 512:
+                nc.scalar.copy(out=h_group[r, n][:, cut:512], in_=src[:, cut:512])
+
+        def quantize_h(r, n):
+            nc.vector.quantize_mx(out=h_codes[r, n][:].bitcast(E5), scales=h_scales[r, n][:], in_=h_group[r, n][:].rearrange("p n t -> p (n t)"))
+
+        def stage2(a, n, b):
+            q, i = a // 2, a % 2
+            acc = bank(b)
+            for r in range(2):
+                m = slice(256 * i + 128 * r, 256 * i + 128 * (r + 1))
+                nc.tensor.matmul_mx(
+                    out=acc[:],
+                    lhsT=v_codes[q][:, m].bitcast(E4),
+                    lhsT_scale=v_scales[q][:, m],
+                    rhs=h_codes[r, n][:].bitcast(E5),
+                    rhs_scale=h_scales[r, n][:],
+                    start=(r == 0),
+                    stop=(r == 1),
+                )
+            return acc
+
+        results = {}
+
+        def empty_out(a, n, acc, engine):
+            q, i = a // 2, a % 2
+            if (q, n) not in results:
+                results[q, n] = work.tile([P, 2, 512], F32, name="result", tag="result", bufs=6, align_bytes=64)
+            dst = results[q, n][:, i, :]
+            if engine == "s":
+                nc.scalar.copy(out=dst, in_=acc[:])
+            else:
+                nc.vector.tensor_copy(out=dst, in_=acc[:])
+
+        def store(q, n):
+            nc.sync.dma_start(out=out_rows[:, 2 * q : 2 * q + 2, 512 * n : 512 * (n + 1)], in_=results[q, n][:])
+
+        for a in range(4):
+            t = transpose_v(a, 4 + a)
+            empty_v(a, t, "s")
+        for g in range(KG):
+            group_u(g, 0, 2)
+            if g == 1:
+                quantize_v(0)
+            if g == 2:
+                quantize_v(1)
+            quantize_u(g, 0)
+            if g == 2:
+                make_gain()
+            stage1(g, 0, 0, 0)
+            stage1(g, 0, 1, 4)
+        for t in range(4):
+            empty_z(0, 0, t, "s")
+        for t in range(2):
+            empty_z(0, 1, t, "s")
+        for g in range(KG):
+            group_u(g, 1, 4 if g < 2 else 2)
+            quantize_u(g, 1)
+            if g == 0:
+                empty_z(0, 1, 2, "v")
+                empty_z(0, 1, 3, "v")
+            stage1(g, 1, 0, 0)
+            stage1(g, 1, 1, 4)
+        group_h(0, 0, 512)
+        quantize_h(0, 0)
+        for t in range(4):
+            empty_z(1, 0, t, "sv"[t % 2])
+        tv = [transpose_v(4 + j, j) for j in range(4)]
+        group_h(1, 0, 344)
+        empty_v(4, tv[0], "s")
+        empty_v(5, tv[1], "s")
+        quantize_h(1, 0)
+        for t in range(4):
+            empty_z(1, 1, t, "s")
+        for j in range(2, 4):
+            empty_v(4 + j, tv[j], "s")
+        group_h(0, 1, 512)
+        quantize_v(2)
+        quantize_h(0, 1)
+        quantize_v(3)
+        group_h(1, 1, 512)
+        quantize_h(1, 1)
+        for blk in range(4):
+            for j in range(4):
+                a = 4 * blk + j
+                acc = stage2(a, 0, 4 + j)
+                empty_out(a, 0, acc, "sv"[j % 2])
+                if j % 2:
+                    store(a // 2, 0)
+            if blk < 2:
+                tv = [transpose_v(8 + 4 * blk + j, j) for j in range(4)]
+                for j in range(4):
+                    empty_v(8 + 4 * blk + j, tv[j], "sv"[j % 2])
+                quantize_v(4 + 2 * blk)
+                quantize_v(5 + 2 * blk)
+        for a in range(ST):
+            acc = stage2(a, 1, a % 8)
+            empty_out(a, 1, acc, "sv"[a % 2])
+            if a % 2:
+                store(a // 2, 1)

@@ -20,6 +20,8 @@ P = 128
 KG = K // 512
 ST = S // P
 SP = ST // 2
+U_CUT = 88
+H_CUT = 256
 
 
 def tile_factored_gain_correction_e3_kernel(tc, innov_words, innov_scales, obs_modes, mode_ratio, state_modes, out):
@@ -53,9 +55,6 @@ def tile_factored_gain_correction_e3_kernel(tc, innov_words, innov_scales, obs_m
 
         make_identity(nc, ident[:])
         nc.vector.memset(g_scales[:].rearrange("p g n -> p (g n)").bitcast(I32), 0)
-        nc.sync.dma_start(out=v_raw[0][:, 0:1, :], in_=v_rows[:, 0:1, :])
-        nc.sync.dma_start(out=v_raw[0][:, 1:2, :], in_=v_rows[:, 1:2, :])
-        nc.sync.dma_start(out=v_raw[1][:], in_=v_rows[:, 2:4, :])
         nc.scalar.dma_start(out=ratio[:], in_=mode_ratio.rearrange("(g p t) -> p g t", g=2, t=4))
         for q in range(4):
             nc.scalar.dma_start(
@@ -67,13 +66,26 @@ def tile_factored_gain_correction_e3_kernel(tc, innov_words, innov_scales, obs_m
             rows = obs_modes[512 * g : 512 * (g + 1), 512 * r : 512 * (r + 1)]
             nc.sync.dma_start(out=u_raw[g, r][:], in_=rows.rearrange("(p j) w -> p j w", j=4))
 
-        for g in range(KG):
-            load_u(g, 0)
+        def load_w(g):
             nc.sync.dma_start(out=g_words[g][:].bitcast(I32), in_=innov_words[g].rearrange("p n t -> p (n t)").bitcast(I32))
+
+        def load_v(q):
+            nc.sync.dma_start(out=v_raw[q][:], in_=v_rows[:, 2 * q : 2 * q + 2, :])
+
+        load_u(0, 0)
+        load_v(0)
+        load_v(1)
+        load_w(0)
+        load_u(1, 0)
+        load_w(1)
+        load_u(2, 0)
+        load_w(2)
+        load_u(3, 0)
+        load_w(3)
         for g in range(KG):
             load_u(g, 1)
         for q in range(2, SP):
-            nc.sync.dma_start(out=v_raw[q][:], in_=v_rows[:, 2 * q : 2 * q + 2, :])
+            load_v(q)
 
         def make_gain():
             flat = ratio[:].rearrange("p g t -> p (g t)")
@@ -84,9 +96,26 @@ def tile_factored_gain_correction_e3_kernel(tc, innov_words, innov_scales, obs_m
 
         v_group = {}
 
+        v_words = {}
+
+        def order_v(q, engine):
+            v_words[q] = work.tile([P, 2, 2, 2, P], F32, name="v_words", tag="v_words", bufs=2, align_bytes=64)
+            src = v_raw[q][:].rearrange("p i r -> p (i r)").bitcast(F32).rearrange("p (x m u) -> p x u m", x=4, u=2)
+            dst = v_words[q][:].rearrange("p i g u m -> p (i g) u m")
+            if engine == "s":
+                nc.scalar.copy(out=dst, in_=src)
+            else:
+                nc.vector.tensor_copy(out=dst, in_=src)
+
         def transpose_v(a, b):
-            words = v_raw[a // 2][:, a % 2, :].bitcast(F32)
             t = bank(b)
+            if a // 2 in v_words:
+                ordered = v_words[a // 2][:, a % 2].rearrange("p g u m -> p (g u m)")
+                for c in range(4):
+                    cols = slice(128 * c, 128 * (c + 1))
+                    nc.tensor.transpose(t[:, cols], ordered[:, cols], ident[:])
+                return t
+            words = v_raw[a // 2][:, a % 2, :].bitcast(F32)
             for g in range(2):
                 for u in range(2):
                     c = 2 * g + u
@@ -109,12 +138,11 @@ def tile_factored_gain_correction_e3_kernel(tc, innov_words, innov_scales, obs_m
 
         u_group = {}
 
-        def group_u(g, r, cut):
-            u_group[g, r] = work.tile([P, 4, P, 4], BF16, name="u_group", tag="u_group", bufs=3, align_bytes=64)
+        def group_u(g, r):
+            u_group[g, r] = work.tile([P, 4, P, 4], BF16, name="u_group", tag="u_group", bufs=4, align_bytes=64)
             src = u_raw[g, r][:].rearrange("p j (m t) -> p t m j", t=4)
-            if cut < 4:
-                nc.scalar.copy(out=u_group[g, r][:, cut:4], in_=src[:, cut:4])
-            nc.vector.tensor_copy(out=u_group[g, r][:, 0:cut], in_=src[:, 0:cut])
+            nc.vector.tensor_copy(out=u_group[g, r][:, :, 0:U_CUT], in_=src[:, :, 0:U_CUT])
+            nc.scalar.copy(out=u_group[g, r][:, :, U_CUT:P], in_=src[:, :, U_CUT:P])
 
         def quantize_u(g, r):
             nc.vector.quantize_mx(out=u_codes[g, r][:].bitcast(E4), scales=u_scales[g, r][:], in_=u_group[g, r][:].rearrange("p t m j -> p (t m j)"))
@@ -149,12 +177,11 @@ def tile_factored_gain_correction_e3_kernel(tc, innov_words, innov_scales, obs_m
             else:
                 nc.vector.tensor_scalar_mul(h_rows[r, n][:, t, :], z[r, n, t][:], scale)
 
-        def group_h(r, n, cut):
+        def group_h(r, n):
             h_group[r, n] = work.tile([P, 512, 4], BF16, name="h_group", tag="h_group", bufs=2, align_bytes=64)
             src = h_rows[r, n][:].rearrange("p t n -> p n t")
-            nc.vector.tensor_copy(out=h_group[r, n][:, 0:cut], in_=src[:, 0:cut])
-            if cut < 512:
-                nc.scalar.copy(out=h_group[r, n][:, cut:512], in_=src[:, cut:512])
+            nc.vector.tensor_copy(out=h_group[r, n][:, 0:H_CUT], in_=src[:, 0:H_CUT])
+            nc.scalar.copy(out=h_group[r, n][:, H_CUT:512], in_=src[:, H_CUT:512])
 
         def quantize_h(r, n):
             nc.vector.quantize_mx(out=h_codes[r, n][:].bitcast(E5), scales=h_scales[r, n][:], in_=h_group[r, n][:].rearrange("p n t -> p (n t)"))
@@ -178,78 +205,108 @@ def tile_factored_gain_correction_e3_kernel(tc, innov_words, innov_scales, obs_m
         results = {}
 
         def empty_out(a, n, acc, engine):
-            q, i = a // 2, a % 2
-            if (q, n) not in results:
-                results[q, n] = work.tile([P, 2, 512], F32, name="result", tag="result", bufs=6, align_bytes=64)
-            dst = results[q, n][:, i, :]
+            if a not in results:
+                results[a] = work.tile([P, 1, N], F32, name="result", tag="result", bufs=6, align_bytes=64)
+            dst = results[a][:, 0, 512 * n : 512 * (n + 1)]
             if engine == "s":
                 nc.scalar.copy(out=dst, in_=acc[:])
             else:
                 nc.vector.tensor_copy(out=dst, in_=acc[:])
 
-        def store(q, n):
-            nc.sync.dma_start(out=out_rows[:, 2 * q : 2 * q + 2, 512 * n : 512 * (n + 1)], in_=results[q, n][:])
+        def store(a):
+            nc.sync.dma_start(out=out_rows[:, a : a + 1, :], in_=results[a][:])
 
+        def stage1_pair(g, r):
+            stage1(g, r, 0, 0)
+            stage1(g, r, 1, 4)
+
+        t = {}
+        group_u(0, 0)
         for a in range(4):
-            t = transpose_v(a, 4 + a)
-            empty_v(a, t, "s")
-        for g in range(KG):
-            group_u(g, 0, 2)
-            if g == 1:
-                quantize_v(0)
-            if g == 2:
-                quantize_v(1)
-            quantize_u(g, 0)
-            if g == 2:
-                make_gain()
-            stage1(g, 0, 0, 0)
-            stage1(g, 0, 1, 4)
-        for t in range(4):
-            empty_z(0, 0, t, "s")
-        for t in range(2):
-            empty_z(0, 1, t, "s")
-        for g in range(KG):
-            group_u(g, 1, 4 if g < 2 else 2)
-            quantize_u(g, 1)
-            if g == 0:
-                empty_z(0, 1, 2, "v")
-                empty_z(0, 1, 3, "v")
-            stage1(g, 1, 0, 0)
-            stage1(g, 1, 1, 4)
-        group_h(0, 0, 512)
+            t[a] = transpose_v(a, 4 + a)
+        quantize_u(0, 0)
+        for a in range(4):
+            empty_v(a, t[a], "s")
+        group_u(1, 0)
+        stage1_pair(0, 0)
+        quantize_v(0)
+        quantize_u(1, 0)
+        make_gain()
+        group_u(2, 0)
+        stage1_pair(1, 0)
+        quantize_v(1)
+        quantize_u(2, 0)
+        group_u(3, 0)
+        stage1_pair(2, 0)
+        quantize_u(3, 0)
+        group_u(0, 1)
+        stage1_pair(3, 0)
+        quantize_u(0, 1)
+        for j in range(4):
+            empty_z(0, 0, j, "s" if j != 1 else "v")
+        group_u(1, 1)
+        for j in range(4):
+            empty_z(0, 1, j, "s" if j != 1 else "v")
+        stage1_pair(0, 1)
+        quantize_u(1, 1)
+        group_u(2, 1)
+        stage1_pair(1, 1)
+        group_h(0, 0)
+        quantize_u(2, 1)
+        group_u(3, 1)
+        stage1_pair(2, 1)
         quantize_h(0, 0)
-        for t in range(4):
-            empty_z(1, 0, t, "sv"[t % 2])
-        tv = [transpose_v(4 + j, j) for j in range(4)]
-        group_h(1, 0, 344)
-        empty_v(4, tv[0], "s")
-        empty_v(5, tv[1], "s")
-        quantize_h(1, 0)
-        for t in range(4):
-            empty_z(1, 1, t, "s")
-        for j in range(2, 4):
-            empty_v(4 + j, tv[j], "s")
-        group_h(0, 1, 512)
-        quantize_v(2)
+        quantize_u(3, 1)
+        group_h(0, 1)
+        stage1_pair(3, 1)
         quantize_h(0, 1)
-        quantize_v(3)
-        group_h(1, 1, 512)
+        for j in range(4):
+            empty_z(1, 0, j, "sv"[j % 2])
+        group_h(1, 0)
+        for a in range(4, 8):
+            t[a] = transpose_v(a, a % 4)
+        for j in range(4):
+            empty_z(1, 1, j, "sv"[j % 2])
+        quantize_h(1, 0)
+        group_h(1, 1)
+        for a in range(4, 8):
+            empty_v(a, t[a], "sv"[a % 2])
+        quantize_v(2)
         quantize_h(1, 1)
-        for blk in range(4):
-            for j in range(4):
-                a = 4 * blk + j
-                acc = stage2(a, 0, 4 + j)
-                empty_out(a, 0, acc, "sv"[j % 2])
-                if j % 2:
-                    store(a // 2, 0)
-            if blk < 2:
-                tv = [transpose_v(8 + 4 * blk + j, j) for j in range(4)]
-                for j in range(4):
-                    empty_v(8 + 4 * blk + j, tv[j], "sv"[j % 2])
-                quantize_v(4 + 2 * blk)
-                quantize_v(5 + 2 * blk)
-        for a in range(ST):
-            acc = stage2(a, 1, a % 8)
-            empty_out(a, 1, acc, "sv"[a % 2])
-            if a % 2:
-                store(a // 2, 1)
+        quantize_v(3)
+
+        def finish(a, n, engine, b):
+            acc = stage2(a, n, b)
+            empty_out(a, n, acc, engine)
+
+        for n in range(2):
+            for a in range(4):
+                finish(a, n, "sv"[a % 2], (4 if n == 0 else 0) + a)
+                if n:
+                    store(a)
+            if n == 0:
+                order_v(4, "v")
+        order_v(5, "v")
+        for blk in (4, 8):
+            ts = list(range(blk + 4, blk + 8))
+            for a in ts:
+                t[a] = transpose_v(a, 4 + a % 4)
+                empty_v(a, t[a], "s")
+            for i in range(4):
+                a = blk + i
+                for n in range(2):
+                    finish(a, n, "vvss"[i], (2 * i + n) % 4)
+                store(a)
+                if i == 1:
+                    if blk == 4:
+                        order_v(6, "v")
+                        order_v(7, "v")
+                    quantize_v(ts[0] // 2)
+                    quantize_v(ts[2] // 2)
+        for a in range(12, ST):
+            for n in range(2):
+                finish(a, n, "sv"[n], (2 * a + n) % 8)
+            if a < ST - 1:
+                store(a)
+        nc.sync.dma_start(out=out_rows[:, ST - 1 : ST, 0:512], in_=results[ST - 1][:, 0:1, 0:512])
+        nc.sync.dma_start(out=out_rows[:, ST - 1 : ST, 512:1024], in_=results[ST - 1][:, 0:1, 512:1024])

@@ -73,18 +73,16 @@ def tile_factored_gain_correction_e3_kernel(tc, innov_words, innov_scales, obs_m
             nc.sync.dma_start(out=v_raw[q][:], in_=v_rows[:, 2 * q : 2 * q + 2, :])
 
         load_u(0, 0)
-        load_v(0)
-        load_v(1)
         load_w(0)
-        load_u(1, 0)
-        load_w(1)
-        load_u(2, 0)
-        load_w(2)
-        load_u(3, 0)
-        load_w(3)
-        for g in range(KG):
+        for g in range(1, KG):
+            load_u(g, 0)
+            if g > 1:
+                load_w(g - 1)
+        load_u(0, 1)
+        load_w(KG - 1)
+        for g in range(1, KG):
             load_u(g, 1)
-        for q in range(2, SP):
+        for q in range(SP):
             load_v(q)
 
         def make_gain():
@@ -204,109 +202,119 @@ def tile_factored_gain_correction_e3_kernel(tc, innov_words, innov_scales, obs_m
 
         results = {}
 
-        def empty_out(a, n, acc, engine):
+        def empty_out(a, n, acc, engine, lo=0, hi=512):
             if a not in results:
                 results[a] = work.tile([P, 1, N], F32, name="result", tag="result", bufs=6, align_bytes=64)
-            dst = results[a][:, 0, 512 * n : 512 * (n + 1)]
+            dst = results[a][:, 0, 512 * n + lo : 512 * n + hi]
             if engine == "s":
-                nc.scalar.copy(out=dst, in_=acc[:])
+                nc.scalar.copy(out=dst, in_=acc[:, lo:hi])
             else:
-                nc.vector.tensor_copy(out=dst, in_=acc[:])
+                nc.vector.tensor_copy(out=dst, in_=acc[:, lo:hi])
 
         def store(a):
             nc.sync.dma_start(out=out_rows[:, a : a + 1, :], in_=results[a][:])
+
+        t = {}
 
         def stage1_pair(g, r):
             stage1(g, r, 0, 0)
             stage1(g, r, 1, 4)
 
-        t = {}
         group_u(0, 0)
-        for a in range(4):
-            t[a] = transpose_v(a, 4 + a)
         quantize_u(0, 0)
-        for a in range(4):
-            empty_v(a, t[a], "s")
-        group_u(1, 0)
-        stage1_pair(0, 0)
-        quantize_v(0)
-        quantize_u(1, 0)
-        make_gain()
-        group_u(2, 0)
-        stage1_pair(1, 0)
-        quantize_v(1)
-        quantize_u(2, 0)
-        group_u(3, 0)
-        stage1_pair(2, 0)
-        quantize_u(3, 0)
+        for g in range(1, KG):
+            group_u(g, 0)
+            stage1_pair(g - 1, 0)
+            if g == 2:
+                make_gain()
+            quantize_u(g, 0)
         group_u(0, 1)
         stage1_pair(3, 0)
         quantize_u(0, 1)
-        for j in range(4):
-            empty_z(0, 0, j, "s" if j != 1 else "v")
+        empty_z(0, 0, 0, "s")
         group_u(1, 1)
-        for j in range(4):
-            empty_z(0, 1, j, "s" if j != 1 else "v")
-        stage1_pair(0, 1)
+        empty_z(0, 1, 0, "s")
+        empty_z(0, 1, 3, "v")
         quantize_u(1, 1)
+        empty_z(0, 1, 1, "s")
+        empty_z(0, 1, 2, "v")
+        stage1(0, 1, 1, 4)
+        stage1(1, 1, 1, 4)
+        empty_z(0, 0, 2, "s")
+        empty_z(0, 0, 3, "s")
         group_u(2, 1)
-        stage1_pair(1, 1)
-        group_h(0, 0)
+        empty_z(0, 0, 1, "v")
         quantize_u(2, 1)
         group_u(3, 1)
-        stage1_pair(2, 1)
-        quantize_h(0, 0)
         quantize_u(3, 1)
+        for g in range(KG):
+            stage1(g, 1, 0, 0)
+        group_h(0, 0)
         group_h(0, 1)
-        stage1_pair(3, 1)
+        for g in range(2, KG):
+            stage1(g, 1, 1, 4)
+        quantize_h(0, 0)
+        order_v(0, "v")
+        for j in range(3):
+            empty_z(1, 0, j, "s")
+        empty_z(1, 0, 3, "v")
+        order_v(1, "v")
         quantize_h(0, 1)
-        for j in range(4):
-            empty_z(1, 0, j, "sv"[j % 2])
         group_h(1, 0)
-        for a in range(4, 8):
-            t[a] = transpose_v(a, a % 4)
         for j in range(4):
-            empty_z(1, 1, j, "sv"[j % 2])
+            empty_z(1, 1, j, "svsv"[j])
+        for a in range(4):
+            t[a] = transpose_v(a, a)
         quantize_h(1, 0)
-        group_h(1, 1)
         for a in range(4, 8):
-            empty_v(a, t[a], "sv"[a % 2])
-        quantize_v(2)
+            t[a] = transpose_v(a, a)
+        empty_v(0, t[0], "s")
+        empty_v(1, t[1], "s")
+        group_h(1, 1)
+        quantize_v(0)
+        empty_v(2, t[2], "v")
+        empty_v(3, t[3], "s")
         quantize_h(1, 1)
-        quantize_v(3)
+        quantize_v(1)
+        empty_v(4, t[4], "s")
+        empty_v(5, t[5], "v")
 
         def finish(a, n, engine, b):
             acc = stage2(a, n, b)
             empty_out(a, n, acc, engine)
 
-        for n in range(2):
-            for a in range(4):
-                finish(a, n, "sv"[a % 2], (4 if n == 0 else 0) + a)
-                if n:
-                    store(a)
-            if n == 0:
+        for i in range(4):
+            for n in range(2):
+                finish(i, n, "sv"[n], (2 * i + n) % 4)
+            store(i)
+            if i == 0:
+                quantize_v(2)
+                empty_v(6, t[6], "s")
+            if i == 1:
+                empty_v(7, t[7], "s")
                 order_v(4, "v")
-        order_v(5, "v")
-        for blk in (4, 8):
-            ts = list(range(blk + 4, blk + 8))
+            if i == 2:
+                quantize_v(3)
+        for q in range(4, SP):
+            ts = (2 * q, 2 * q + 1)
             for a in ts:
                 t[a] = transpose_v(a, 4 + a % 4)
                 empty_v(a, t[a], "s")
-            for i in range(4):
-                a = blk + i
+            for i in range(2):
+                a = 2 * q - 4 + i
                 for n in range(2):
-                    finish(a, n, "vvss"[i], (2 * i + n) % 4)
+                    finish(a, n, "vs"[n], (2 * a + n) % 4)
                 store(a)
-                if i == 1:
-                    if blk == 4:
-                        order_v(6, "v")
-                        order_v(7, "v")
-                    quantize_v(ts[0] // 2)
-                    quantize_v(ts[2] // 2)
-        for a in range(12, ST):
+                if i == 0 and q + 1 < SP:
+                    order_v(q + 1, "v")
+            quantize_v(q)
+        for a in range(ST - 4, ST - 1):
             for n in range(2):
                 finish(a, n, "sv"[n], (2 * a + n) % 8)
-            if a < ST - 1:
-                store(a)
-        nc.sync.dma_start(out=out_rows[:, ST - 1 : ST, 0:512], in_=results[ST - 1][:, 0:1, 0:512])
-        nc.sync.dma_start(out=out_rows[:, ST - 1 : ST, 512:1024], in_=results[ST - 1][:, 0:1, 512:1024])
+            store(a)
+        last = ST - 1
+        for n in range(2):
+            acc = stage2(last, n, 6 + n)
+            empty_out(last, n, acc, "s", 0, 256)
+            empty_out(last, n, acc, "v", 256, 512)
+            nc.sync.dma_start(out=out_rows[:, last : ST, 512 * n : 512 * (n + 1)], in_=results[last][:, 0:1, 512 * n : 512 * (n + 1)])

@@ -138,9 +138,10 @@ def tile_factored_gain_correction_e3_kernel(tc, innov_words, innov_scales, obs_m
 
         def group_u(g, r):
             u_group[g, r] = work.tile([P, 4, P, 4], BF16, name="u_group", tag="u_group", bufs=4, align_bytes=64)
-            src = u_raw[g, r][:].rearrange("p j (m t) -> p t m j", t=4)
-            nc.vector.tensor_copy(out=u_group[g, r][:, :, 0:U_CUT], in_=src[:, :, 0:U_CUT])
-            nc.scalar.copy(out=u_group[g, r][:, :, U_CUT:P], in_=src[:, :, U_CUT:P])
+            src = u_raw[g, r][:].rearrange("p j (m t) -> p m j t", t=4)
+            dst = u_group[g, r][:].rearrange("p t m j -> p m j t")
+            nc.vector.tensor_copy(out=dst[:, 0:U_CUT], in_=src[:, 0:U_CUT])
+            nc.scalar.copy(out=dst[:, U_CUT:P], in_=src[:, U_CUT:P])
 
         def quantize_u(g, r):
             nc.vector.quantize_mx(out=u_codes[g, r][:].bitcast(E4), scales=u_scales[g, r][:], in_=u_group[g, r][:].rearrange("p t m j -> p (t m j)"))
@@ -177,9 +178,11 @@ def tile_factored_gain_correction_e3_kernel(tc, innov_words, innov_scales, obs_m
 
         def group_h(r, n):
             h_group[r, n] = work.tile([P, 512, 4], BF16, name="h_group", tag="h_group", bufs=2, align_bytes=64)
-            src = h_rows[r, n][:].rearrange("p t n -> p n t")
-            nc.vector.tensor_copy(out=h_group[r, n][:, 0:H_CUT], in_=src[:, 0:H_CUT])
-            nc.scalar.copy(out=h_group[r, n][:, H_CUT:512], in_=src[:, H_CUT:512])
+            src = h_rows[r, n][:].rearrange("p t (c i) -> p c t i", i=4)
+            dst = h_group[r, n][:].rearrange("p (c i) t -> p c t i", i=4)
+            cut = H_CUT // 4
+            nc.vector.tensor_copy(out=dst[:, 0:cut], in_=src[:, 0:cut])
+            nc.scalar.copy(out=dst[:, cut:P], in_=src[:, cut:P])
 
         def quantize_h(r, n):
             nc.vector.quantize_mx(out=h_codes[r, n][:].bitcast(E5), scales=h_scales[r, n][:], in_=h_group[r, n][:].rearrange("p n t -> p (n t)"))
@@ -229,21 +232,22 @@ def tile_factored_gain_correction_e3_kernel(tc, innov_words, innov_scales, obs_m
                 make_gain()
             quantize_u(g, 0)
         group_u(0, 1)
-        stage1_pair(3, 0)
-        quantize_u(0, 1)
-        empty_z(0, 0, 0, "s")
-        group_u(1, 1)
+        stage1(3, 0, 1, 4)
+        stage1(3, 0, 0, 0)
         empty_z(0, 1, 0, "s")
-        empty_z(0, 1, 3, "v")
+        quantize_u(0, 1)
+        empty_z(0, 1, 2, "s")
+        empty_z(0, 1, 1, "v")
+        group_u(1, 1)
+        empty_z(0, 1, 3, "s")
         quantize_u(1, 1)
-        empty_z(0, 1, 1, "s")
-        empty_z(0, 1, 2, "v")
         stage1(0, 1, 1, 4)
         stage1(1, 1, 1, 4)
-        empty_z(0, 0, 2, "s")
-        empty_z(0, 0, 3, "s")
-        group_u(2, 1)
+        empty_z(0, 0, 0, "s")
         empty_z(0, 0, 1, "v")
+        empty_z(0, 0, 2, "s")
+        group_u(2, 1)
+        empty_z(0, 0, 3, "s")
         quantize_u(2, 1)
         group_u(3, 1)
         quantize_u(3, 1)

from contextlib import ExitStack

import concourse.mybir as mybir
from concourse.masks import make_identity

K, N, R, S = 2048, 1024, 1024, 2048
FLOPS = 2 * K * R * N + 2 * S * R * N

F32 = mybir.dt.float32
BF16 = mybir.dt.bfloat16
U32 = mybir.dt.uint32
I32 = mybir.dt.int32
U8 = mybir.dt.uint8
E4 = mybir.dt.float8_e4m3fn_x4
E5 = mybir.dt.float8_e5m2_x4
COPY = mybir.ActivationFunctionType.Copy
MULT = mybir.AluOpType.mult

P = 128
KG = K // 512
ST = S // P
SP = ST // 2
U_CUT = 88
H_CUT = 256


def tile_factored_gain_correction_e3_kernel(tc, innov_words, innov_scales, obs_modes, mode_ratio, state_modes, out):
    nc = tc.nc
    v_rows = state_modes.rearrange("(p a) r -> p a r", a=ST)
    out_rows = out.rearrange("(p a) n -> p a n", a=ST)

    with ExitStack() as ctx:
        keep = ctx.enter_context(tc.tile_pool(name="keep", bufs=1))
        work = ctx.enter_context(tc.tile_pool(name="work", bufs=2))
        psum = ctx.enter_context(tc.psum_pool(name="psum", bufs=1))
        ctx.enter_context(tc.manual_schedule())

        def bank(b):
            return psum.tile([P, 512], F32, name="bank%d" % b, tag="bank%d" % b)

        ident = keep.tile([P, P], F32, name="ident", align_bytes=64)
        ratio = keep.tile([P, 2, 4], BF16, name="ratio")
        square = keep.tile([P, 8], F32, name="square")
        gain = keep.tile([P, 8], F32, name="gain")
        g_words = [keep.tile([P, N], U32, name="g_words%d" % g, align_bytes=64) for g in range(KG)]
        g_scales = keep.tile([P, KG, N], U8, name="g_scales", align_bytes=64)
        u_raw = {(g, r): keep.tile([P, 4, 512], BF16, name="u_raw%d_%d" % (g, r), align_bytes=64) for g in range(KG) for r in range(2)}
        u_codes = {k: keep.tile([P, 512], U32, name="u_codes%d_%d" % k, align_bytes=64) for k in u_raw}
        u_scales = {k: keep.tile([P, 512], U8, name="u_scales%d_%d" % k, align_bytes=64) for k in u_raw}
        v_raw = [keep.tile([P, 2, R], BF16, name="v_raw%d" % q, align_bytes=64) for q in range(SP)]
        v_codes = [keep.tile([P, 512], U32, name="v_codes%d" % q, align_bytes=64) for q in range(SP)]
        v_scales = [keep.tile([P, 512], U8, name="v_scales%d" % q, align_bytes=64) for q in range(SP)]
        h_codes = {(r, n): keep.tile([P, 512], U32, name="h_codes%d_%d" % (r, n), align_bytes=64) for r in range(2) for n in range(2)}
        h_scales = {k: keep.tile([P, 512], U8, name="h_scales%d_%d" % k, align_bytes=64) for k in h_codes}

        make_identity(nc, ident[:])
        nc.vector.memset(g_scales[:].rearrange("p g n -> p (g n)").bitcast(I32), 0)
        nc.scalar.dma_start(out=ratio[:], in_=mode_ratio.rearrange("(g p t) -> p g t", g=2, t=4))
        for q in range(4):
            nc.scalar.dma_start(
                out=g_scales[32 * q : 32 * q + 4, :, :].bitcast(I32),
                in_=innov_scales[:, 4 * q : 4 * q + 4, :].rearrange("g q n -> q g n").bitcast(I32),
            )

        def load_u(g, r):
            rows = obs_modes[512 * g : 512 * (g + 1), 512 * r : 512 * (r + 1)]
            nc.sync.dma_start(out=u_raw[g, r][:], in_=rows.rearrange("(p j) w -> p j w", j=4))

        def load_w(g):
            nc.sync.dma_start(out=g_words[g][:].bitcast(I32), in_=innov_words[g].rearrange("p n t -> p (n t)").bitcast(I32))

        def load_v(q):
            nc.sync.dma_start(out=v_raw[q][:], in_=v_rows[:, 2 * q : 2 * q + 2, :])

        load_u(0, 0)
        load_w(0)
        for g in range(1, KG):
            load_u(g, 0)
            if g > 1:
                load_w(g - 1)
        load_u(0, 1)
        load_w(KG - 1)
        for g in range(1, KG):
            load_u(g, 1)
        for q in range(SP):
            load_v(q)

        def make_gain():
            flat = ratio[:].rearrange("p g t -> p (g t)")
            nc.vector.tensor_tensor(out=square[:], in0=flat, in1=flat, op=MULT)
            nc.vector.tensor_scalar_add(square[:], square[:], 1.0)
            nc.vector.reciprocal(square[:], square[:])
            nc.vector.tensor_tensor(out=gain[:], in0=flat, in1=square[:], op=MULT)

        v_group = {}

        v_words = {}

        def order_v(q, engine):
            v_words[q] = work.tile([P, 2, 2, 2, P], F32, name="v_words", tag="v_words", bufs=2, align_bytes=64)
            src = v_raw[q][:].rearrange("p i r -> p (i r)").bitcast(F32).rearrange("p (x m u) -> p x u m", x=4, u=2)
            dst = v_words[q][:].rearrange("p i g u m -> p (i g) u m")
            if engine == "s":
                nc.scalar.copy(out=dst, in_=src)
            else:
                nc.vector.tensor_copy(out=dst, in_=src)

        def transpose_v(a, b):
            t = bank(b)
            if a // 2 in v_words:
                ordered = v_words[a // 2][:, a % 2].rearrange("p g u m -> p (g u m)")
                for c in range(4):
                    cols = slice(128 * c, 128 * (c + 1))
                    nc.tensor.transpose(t[:, cols], ordered[:, cols], ident[:])
                return t
            words = v_raw[a // 2][:, a % 2, :].bitcast(F32)
            for g in range(2):
                for u in range(2):
                    c = 2 * g + u
                    nc.tensor.transpose(t[:, 128 * c : 128 * (c + 1)], words[:, 256 * g + u : 256 * (g + 1) : 2], ident[:])
            return t

        def empty_v(a, t, engine):
            q = a // 2
            if q not in v_group:
                v_group[q] = work.tile([P, 2, 2, P, 4], BF16, name="v_group", tag="v_group", bufs=3, align_bytes=64)
            dst = v_group[q][:, a % 2].rearrange("p g s t -> p g (s t)").bitcast(F32).rearrange("p g (s u) -> p g s u", u=2)
            src = t[:].rearrange("p (g u s) -> p g s u", g=2, u=2)
            if engine == "s":
                nc.scalar.copy(out=dst, in_=src)
            else:
                nc.vector.tensor_copy(out=dst, in_=src)

        def quantize_v(q):
            nc.vector.quantize_mx(out=v_codes[q][:].bitcast(E4), scales=v_scales[q][:], in_=v_group[q][:].rearrange("p i g s t -> p (i g s t)"))

        u_group = {}

        def group_u(g, r):
            u_group[g, r] = work.tile([P, 4, P, 4], BF16, name="u_group", tag="u_group", bufs=4, align_bytes=64)
            src = u_raw[g, r][:].rearrange("p j (m t) -> p m j t", t=4)
            dst = u_group[g, r][:].rearrange("p t m j -> p m j t")
            nc.vector.tensor_copy(out=dst[:, 0:U_CUT], in_=src[:, 0:U_CUT])
            nc.scalar.copy(out=dst[:, U_CUT:P], in_=src[:, U_CUT:P])

        def quantize_u(g, r):
            nc.vector.quantize_mx(out=u_codes[g, r][:].bitcast(E4), scales=u_scales[g, r][:], in_=u_group[g, r][:].rearrange("p t m j -> p (t m j)"))

        z = {}

        def stage1(g, r, n, base):
            cols = slice(512 * n, 512 * (n + 1))
            for t in range(4):
                if g == 0:
                    z[r, n, t] = bank(base + t)
                m = slice(128 * t, 128 * (t + 1))
                nc.tensor.matmul_mx(
                    out=z[r, n, t][:],
                    lhsT=u_codes[g, r][:, m].bitcast(E4),
                    lhsT_scale=u_scales[g, r][:, m],
                    rhs=g_words[g][:, cols].bitcast(E5),
                    rhs_scale=g_scales[:, g, cols],
                    start=(g == 0),
                    stop=(g == KG - 1),
                )

        h_rows = {}
        h_group = {}

        def empty_z(r, n, t, engine):
            if (r, n) not in h_rows:
                h_rows[r, n] = work.tile([P, 4, 512], BF16, name="h_rows", tag="h_rows", bufs=3, align_bytes=64)
            scale = gain[:, 4 * r + t : 4 * r + t + 1]
            if engine == "s":
                nc.scalar.activation(out=h_rows[r, n][:, t, :], in_=z[r, n, t][:], func=COPY, scale=scale)
            else:
                nc.vector.tensor_scalar_mul(h_rows[r, n][:, t, :], z[r, n, t][:], scale)

        def group_h(r, n):
            h_group[r, n] = work.tile([P, 512, 4], BF16, name="h_group", tag="h_group", bufs=2, align_bytes=64)
            src = h_rows[r, n][:].rearrange("p t (c i) -> p c t i", i=4)
            dst = h_group[r, n][:].rearrange("p (c i) t -> p c t i", i=4)
            cut = H_CUT // 4
            nc.vector.tensor_copy(out=dst[:, 0:cut], in_=src[:, 0:cut])
            nc.scalar.copy(out=dst[:, cut:P], in_=src[:, cut:P])

        def quantize_h(r, n):
            nc.vector.quantize_mx(out=h_codes[r, n][:].bitcast(E5), scales=h_scales[r, n][:], in_=h_group[r, n][:].rearrange("p n t -> p (n t)"))

        def stage2(a, n, b):
            q, i = a // 2, a % 2
            acc = bank(b)
            for r in range(2):
                m = slice(256 * i + 128 * r, 256 * i + 128 * (r + 1))
                nc.tensor.matmul_mx(
                    out=acc[:],
                    lhsT=v_codes[q][:, m].bitcast(E4),
                    lhsT_scale=v_scales[q][:, m],
                    rhs=h_codes[r, n][:].bitcast(E5),
                    rhs_scale=h_scales[r, n][:],
                    start=(r == 0),
                    stop=(r == 1),
                )
            return acc

        results = {}

        def empty_out(a, n, acc, engine, lo=0, hi=512):
            if a not in results:
                results[a] = work.tile([P, 1, N], F32, name="result", tag="result", bufs=6, align_bytes=64)
            dst = results[a][:, 0, 512 * n + lo : 512 * n + hi]
            if engine == "s":
                nc.scalar.copy(out=dst, in_=acc[:, lo:hi])
            else:
                nc.vector.tensor_copy(out=dst, in_=acc[:, lo:hi])

        def store(a):
            nc.sync.dma_start(out=out_rows[:, a : a + 1, :], in_=results[a][:])

        t = {}

        def stage1_pair(g, r):
            stage1(g, r, 0, 0)
            stage1(g, r, 1, 4)

        group_u(0, 0)
        quantize_u(0, 0)
        for g in range(1, KG):
            group_u(g, 0)
            stage1_pair(g - 1, 0)
            if g == 2:
                make_gain()
            quantize_u(g, 0)
        group_u(0, 1)
        stage1(3, 0, 1, 4)
        stage1(3, 0, 0, 0)
        empty_z(0, 1, 0, "s")
        quantize_u(0, 1)
        empty_z(0, 1, 2, "s")
        empty_z(0, 1, 1, "v")
        group_u(1, 1)
        empty_z(0, 1, 3, "s")
        quantize_u(1, 1)
        stage1(0, 1, 1, 4)
        stage1(1, 1, 1, 4)
        empty_z(0, 0, 0, "s")
        empty_z(0, 0, 1, "v")
        empty_z(0, 0, 2, "s")
        group_u(2, 1)
        empty_z(0, 0, 3, "s")
        quantize_u(2, 1)
        group_u(3, 1)
        quantize_u(3, 1)
        for g in range(KG):
            stage1(g, 1, 0, 0)
        group_h(0, 0)
        group_h(0, 1)
        for g in range(2, KG):
            stage1(g, 1, 1, 4)
        quantize_h(0, 0)
        order_v(0, "v")
        for j in range(3):
            empty_z(1, 0, j, "s")
        empty_z(1, 0, 3, "v")
        order_v(1, "v")
        quantize_h(0, 1)
        group_h(1, 0)
        for j in range(4):
            empty_z(1, 1, j, "svsv"[j])
        for a in range(4):
            t[a] = transpose_v(a, a)
        quantize_h(1, 0)
        for a in range(4, 8):
            t[a] = transpose_v(a, a)
        empty_v(0, t[0], "s")
        empty_v(1, t[1], "s")
        group_h(1, 1)
        quantize_v(0)
        empty_v(2, t[2], "v")
        empty_v(3, t[3], "s")
        quantize_h(1, 1)
        quantize_v(1)
        empty_v(4, t[4], "s")
        empty_v(5, t[5], "v")

        def finish(a, n, engine, b):
            acc = stage2(a, n, b)
            empty_out(a, n, acc, engine)

        for i in range(4):
            for n in range(2):
                finish(i, n, "sv"[n], (2 * i + n) % 4)
            store(i)
            if i == 0:
                quantize_v(2)
                empty_v(6, t[6], "s")
            if i == 1:
                empty_v(7, t[7], "s")
                order_v(4, "v")
            if i == 2:
                quantize_v(3)
        for q in range(4, SP):
            ts = (2 * q, 2 * q + 1)
            for a in ts:
                t[a] = transpose_v(a, 4 + a % 4)
                empty_v(a, t[a], "s")
            for i in range(2):
                a = 2 * q - 4 + i
                for n in range(2):
                    finish(a, n, "vs"[n], (2 * a + n) % 4)
                store(a)
                if i == 0 and q + 1 < SP:
                    order_v(q + 1, "v")
            quantize_v(q)
        for a in range(ST - 4, ST - 1):
            for n in range(2):
                finish(a, n, "sv"[n], (2 * a + n) % 8)
            store(a)
        last = ST - 1
        for n in range(2):
            acc = stage2(last, n, 6 + n)
            empty_out(last, n, acc, "s", 0, 256)
            empty_out(last, n, acc, "v", 256, 512)
            nc.sync.dma_start(out=out_rows[:, last : ST, 512 * n : 512 * (n + 1)], in_=results[last][:, 0:1, 512 * n : 512 * (n + 1)])
